import numpy as np
import ml_dtypes


def mxq(x, axis, fmt="e4m3"):
    dtype, down = {"e4m3": (ml_dtypes.float8_e4m3fn, 7), "e5m2": (ml_dtypes.float8_e5m2, 14)}[fmt]
    v = np.moveaxis(np.asarray(x, np.float32).astype(ml_dtypes.bfloat16).astype(np.float64), axis, -1)
    blocks = v.reshape(v.shape[:-1] + (-1, 32))
    amax = np.abs(blocks).max(-1, keepdims=True)
    byte = np.maximum(np.where(amax > 0, np.frexp(amax)[1] - 1 + 127, 0) - down, 1)
    scale = np.exp2(byte - 127.0)
    codes = (blocks / scale).astype(np.float32).astype(dtype).astype(np.float64)
    return np.moveaxis((codes * scale).reshape(v.shape), -1, axis)


WIDE = False


def mx_kscale(k):
    if not WIDE:
        return np.ones(k)
    levels = np.array([10, -10, 5, -5, 0])
    if k % 512:
        return np.exp2(np.random.permutation(np.resize(levels, k // 32))).repeat(32)
    a = np.empty((k // 512, 16))
    for p in range(k // 512):
        a[p, :8] = np.random.permutation(np.resize(levels, 8))
        for g in range(8):
            far = levels[np.abs(levels - a[p, g]) >= 10]
            a[p, g + 8] = far[np.random.randint(len(far))]
    return np.exp2(a.ravel()).repeat(32)


BF16 = ml_dtypes.bfloat16


def bf(x):
    return np.asarray(x, np.float32).astype(BF16)


def f64(x):
    return np.asarray(x).astype(np.float64)


E2M1 = np.array([0.0, 0.5, 1.0, 1.5, 2.0, 3.0, 4.0, 6.0, -0.0, -0.5, -1.0, -1.5, -2.0, -3.0, -4.0, -6.0])


def pack_weight(w, fmt):
    k, n = w.shape
    w = f64(bf(w)).reshape(k // 32, 32, n)
    amax = np.abs(w).max(1)
    if fmt == "e4m3":
        byte = np.frexp(amax)[1] - 1 + 127 - 7
    else:
        mant, ex = np.frexp(amax / 6.0)
        byte = np.where(mant > 0.5, ex, ex - 1) + 127
    byte = np.clip(np.where(amax > 0, byte, 1), 1, 254)
    scaled = (w * np.exp2(127.0 - byte)[:, None, :]).reshape(k, n).astype(np.float32)
    by_word = np.ascontiguousarray(scaled.reshape(k // 512, 128, 4, n).transpose(0, 1, 3, 2))
    if fmt == "e4m3":
        words = by_word.astype(ml_dtypes.float8_e4m3fn).view(np.uint8)
    else:
        c = by_word.astype(ml_dtypes.float4_e2m1fn).view(np.uint8) & 0xF
        words = c[..., 0::2] | (c[..., 1::2] << 4)
    return np.ascontiguousarray(words), np.ascontiguousarray(byte.astype(np.uint8).reshape(k // 512, 16, n))


def unpack_weight(words, scales, fmt):
    g, p, n, _ = words.shape
    if fmt == "e4m3":
        vals = np.ascontiguousarray(words).view(ml_dtypes.float8_e4m3fn).astype(np.float64)
    else:
        nib = np.empty((g, p, n, 4), np.uint8)
        nib[..., 0::2] = words & 0xF
        nib[..., 1::2] = words >> 4
        vals = E2M1[nib]
    vals = vals * np.repeat(np.exp2(scales.astype(np.float64) - 127.0), 8, axis=1)[..., None]
    return vals.transpose(0, 1, 3, 2).reshape(g * 512, n)
def pack4(w):
    words, scales = pack_weight(w, "e2m1")
    return words.reshape(words.shape[0], 128, -1), scales


def unpack4(words, scales):
    return unpack_weight(words.reshape(words.shape[0], 128, -1, 2), scales, "e2m1")


E4M3FN = np.array([(-1.0 if i & 128 else 1.0) * ((1.0 + (i & 7) / 8.0) * 2.0 ** (((i >> 3) & 15) - 7) if i & 120 else (i & 7) * 2.0 ** -9) for i in range(256)])


def e4m3fn_bytes(y):
    return np.clip(np.asarray(y, np.float64), -448.0, 448.0).astype(np.float32).astype(ml_dtypes.float8_e4m3fn).view(np.uint8)


def e4m3fn_values(b):
    return E4M3FN[b]


K, B, N, M, E = 2, 512, 1024, 1024, 4


def draw0():
    u, t = mx_kscale(N), mx_kscale(M)
    mat = np.random.standard_normal((K, B, N)) * 0.3 * u
    a = np.random.standard_normal((N, M)) / np.sqrt(N) / u[:, None]
    f = np.random.uniform(0.3, 1.2, (K, E))
    s = np.random.uniform(0.2, 0.6, (E,))
    y = np.random.uniform(0.5, 2.5, (B, M))
    w = (1.0 + 0.1 * np.random.standard_normal(M)) * t
    q = np.random.standard_normal((M, N)) / np.sqrt(M) / t[:, None]
    a_words, a_scales = pack4(a)
    q_words, q_scales = pack4(q)
    return {"mat": bf(mat), "a_words": a_words, "a_scales": a_scales, "f": bf(f), "s": bf(s), "y": bf(y), "w": bf(w), "q_words": q_words, "q_scales": q_scales}


def transmitted_spectrum(l, f, s):
    attenuation = np.sum(f[:, :, None, None] * l[:, None, :, :], axis=0)
    return s[:, None, None] * np.exp(-attenuation)


def core(mat, a_words, a_scales, f, s, y, w, q_words, q_scales):
    f, s, y, w = f64(f), f64(s), f64(y), f64(w)
    l = mxq(f64(mat), 2, "e4m3") @ unpack4(a_words, a_scales)
    t = transmitted_spectrum(l, f, s)
    ybar = np.sum(t, axis=0)
    c = np.sum(f[:, :, None, None] * t[None, :, :, :], axis=1)
    residual = w[None, :] * (1.0 - y / ybar)
    g = residual[None, :, :] * c
    return mxq(g, 2, "e4m3") @ unpack4(q_words, q_scales)


def setup_inputs():
    drawn = draw0()
    full = np.asarray(drawn['mat']).astype(np.float64)
    scale = (np.abs(full).reshape(2, 512, 8, 128).max(axis=(3,)) / 448.0).astype(np.float32)
    given = {}
    for key, value in drawn.items():
        if key == 'mat':
            given['mat_bytes'] = e4m3fn_bytes(full / np.repeat(scale.astype(np.float64), 128, axis=2))
            given['mat_scale'] = scale
        else:
            given[key] = value
    return given


def reference(mat_bytes, mat_scale, a_words, a_scales, f, s, y, w, q_words, q_scales):
    return core(e4m3fn_values(mat_bytes) * np.repeat(mat_scale.astype(np.float64), 128, axis=2), a_words, a_scales, f, s, y, w, q_words, q_scales)

@@ -1,0 +1,386 @@
+from contextlib import ExitStack
+
+import concourse.mybir as mybir
+from concourse.masks import make_identity
+
+MATS, B, N, M, E = 2, 512, 1024, 1024, 4
+FLOPS = 2 * 2 * MATS * B * N * M
+
+F32 = mybir.dt.float32
+BF16 = mybir.dt.bfloat16
+I32 = mybir.dt.int32
+U32 = mybir.dt.uint32
+U8 = mybir.dt.uint8
+FP8 = mybir.dt.float8_e4m3fn
+FP8X4 = mybir.dt.float8_e4m3fn_x4
+FP4X4 = mybir.dt.float4_e2m1fn_x4
+ALU = mybir.AluOpType
+ACT = mybir.ActivationFunctionType
+
+P = 128
+TILES = B // P
+TINY = 2.0**-100
+POOL_PRODUCTS = ((1, 0), (1, 1), (1, 2), (2, 0), (2, 1), (2, 2))
+SCALAR_PRODUCTS = ((3, 0), (3, 1), (3, 2))
+
+
+def tile_polyenergetictwomaterialunmatchedbackpro_d1p_kernel(
+    tc, mat_bytes, mat_scale, a_words, a_scales, f, s, y, w, q_words, q_scales, out
+):
+    nc = tc.nc
+    with ExitStack() as ctx:
+        keep = ctx.enter_context(tc.tile_pool(name="keep", bufs=1))
+        load = ctx.enter_context(tc.tile_pool(name="load", bufs=4))
+        work = ctx.enter_context(tc.tile_pool(name="work", bufs=2))
+        deep = ctx.enter_context(tc.tile_pool(name="deep", bufs=3))
+        pmisc = ctx.enter_context(tc.psum_pool(name="pmisc", bufs=2))
+        pl = ctx.enter_context(tc.psum_pool(name="pl", bufs=3))
+        pz = ctx.enter_context(tc.psum_pool(name="pz", bufs=3))
+
+        ident = keep.tile([P, P], F32, name="ident")
+        make_identity(nc, ident[:])
+        a_sc = keep.tile([P, 2, M], U8, name="a_sc", align_bytes=64)
+        q_sc = keep.tile([P, 2, N], U8, name="q_sc", align_bytes=64)
+        nc.vector.memset(a_sc[:].rearrange("p g n -> p (g n)").bitcast(I32), 0)
+        nc.vector.memset(q_sc[:].rearrange("p g n -> p (g n)").bitcast(I32), 0)
+        a_sb = keep.tile([P, 2, 2 * M], U8, name="a_sb", align_bytes=64)
+        q_sb = keep.tile([P, 2, 2 * N], U8, name="q_sb", align_bytes=64)
+
+        warm = keep.tile([P, 1], F32, name="warm")
+        nc.vector.memset(warm[:], 0.0)
+        nc.scalar.activation(out=warm[:], in_=warm[:], func=ACT.Exp)
+        raw, scl, ynat = [], [], []
+
+        def load_mat(i):
+            rows = slice(P * i, P * (i + 1))
+            sc = load.tile([P, MATS, 8], F32, name="sc")
+            nc.sync.dma_start(out=sc[:], in_=mat_scale[:, rows, :].rearrange("k b j -> b k j"))
+            rb = load.tile([P, MATS, N], U8, name="rb")
+            nc.sync.dma_start(out=rb[:], in_=mat_bytes[:, rows, :].rearrange("k b n -> b k n"))
+            scl.append(sc)
+            raw.append(rb)
+
+        def load_y(i):
+            yt = load.tile([P, M], BF16, name="yt")
+            nc.sync.dma_start(out=yt[:], in_=y[P * i : P * (i + 1), :])
+            ynat.append(yt)
+
+        def load_scales(dst, src):
+            for q in range(4):
+                nc.sync.dma_start(
+                    out=dst[32 * q : 32 * q + 4, :, :].bitcast(I32),
+                    in_=src[:, 4 * q : 4 * q + 4, :].bitcast(I32).rearrange("g r n -> r g n"),
+                )
+
+        load_mat(0)
+        f_bf = keep.tile([P, MATS * E], BF16, name="f_bf")
+        nc.sync.dma_start(out=f_bf[:], in_=f.rearrange("k e -> (k e)").partition_broadcast(P))
+        s_bf = keep.tile([P, E], BF16, name="s_bf")
+        nc.sync.dma_start(out=s_bf[:], in_=s.partition_broadcast(P))
+        load_scales(a_sc, a_scales)
+        for g in range(2):
+            nc.sync.dma_start(out=a_sb[:, g, :].bitcast(I32), in_=a_words[g].bitcast(I32))
+        load_mat(1)
+        load_y(0)
+        w_sb = keep.tile([P, 2, 4], BF16, name="w_sb")
+        nc.sync.dma_start(out=w_sb[:], in_=w.rearrange("(g p t) -> p g t", g=2, t=4))
+        load_scales(q_sc, q_scales)
+        for g in range(2):
+            nc.sync.dma_start(out=q_sb[:, g, :].bitcast(I32), in_=q_words[g].bitcast(I32))
+        load_y(1)
+        for i in range(2, TILES):
+            load_mat(i)
+            load_y(i)
+
+        fx = keep.tile([P, MATS * E], F32, name="fx")
+        sx = keep.tile([P, E], F32, name="sx")
+        fs = keep.tile([P, MATS, E], F32, name="fs")
+        norm = keep.tile([P, 7], F32, name="norm")
+        mag = keep.tile([P, 7], F32, name="mag")
+        bump = keep.tile([P, 7], F32, name="bump")
+        lead = keep.tile([P, 7], F32, name="lead")
+        inv = keep.tile([P, 7], F32, name="inv")
+        rho = keep.tile([P, E], F32, name="rho")
+        neg = keep.tile([P, 7], F32, name="neg")
+        gsc = keep.tile([P, MATS], F32, name="gsc")
+        coef = keep.tile([P, 3, E], F32, name="coef")
+
+        def coefficients():
+            nc.vector.tensor_copy(out=fx[:], in_=f_bf[:])
+            nc.vector.tensor_copy(out=sx[:], in_=s_bf[:])
+            nc.vector.tensor_tensor(
+                out=fs[:],
+                in0=fx[:].rearrange("p (k e) -> p k e", k=MATS),
+                in1=sx[:].unsqueeze(1).to_broadcast([P, MATS, E]),
+                op=ALU.mult,
+            )
+            nc.vector.tensor_copy(out=norm[:, 0:4], in_=fx[:, 0:4])
+            nc.vector.tensor_copy(out=norm[:, 4:5], in_=sx[:, 0:1])
+            nc.vector.tensor_copy(out=norm[:, 5:7], in_=fs[:, :, 0])
+            nc.vector.scalar_tensor_tensor(out=mag[:], in0=norm[:], scalar=-1.0, in1=norm[:], op0=ALU.mult, op1=ALU.max)
+            nc.vector.tensor_scalar(out=bump[:], in0=mag[:], scalar1=TINY, scalar2=TINY, op0=ALU.is_lt, op1=ALU.mult)
+            nc.vector.tensor_tensor(out=lead[:], in0=norm[:], in1=bump[:], op=ALU.add)
+            nc.vector.reciprocal(out=inv[:], in_=lead[:])
+            nc.vector.tensor_tensor(out=rho[:], in0=fx[:, 4:8], in1=inv[:, 0:4], op=ALU.mult)
+            nc.vector.tensor_scalar(out=neg[:], in0=lead[:], scalar1=-1.0, scalar2=None, op0=ALU.mult)
+            nc.vector.tensor_scalar(out=gsc[:], in0=neg[:, 5:7], scalar1=inv[:, 4:5], scalar2=None, op0=ALU.mult)
+            nc.vector.tensor_scalar(out=coef[:, 0, :], in0=sx[:], scalar1=inv[:, 4:5], scalar2=None, op0=ALU.mult)
+            for k in range(MATS):
+                nc.vector.tensor_scalar(
+                    out=coef[:, 1 + k, :], in0=fs[:, k, :], scalar1=inv[:, 5 + k : 6 + k], scalar2=None, op0=ALU.mult
+                )
+
+
+        nats, groups, codes, planes, yturned = {}, {}, {}, {}, {}
+
+        def widen(i, k, engine):
+            if i not in nats:
+                nats[i] = work.tile([P, MATS, N], BF16, name="nat")
+            nat = nats[i]
+            for j in range(8):
+                cols = slice(P * j, P * (j + 1))
+                src = raw[i][:, k, cols].bitcast(FP8)
+                if engine == "a":
+                    nc.scalar.activation(out=nat[:, k, cols], in_=src, func=ACT.Copy, scale=scl[i][:, k, j : j + 1])
+                else:
+                    nc.vector.tensor_scalar(
+                        out=nat[:, k, cols], in0=src, scalar1=scl[i][:, k, j : j + 1], scalar2=None, op0=ALU.mult
+                    )
+
+        def turn(src_words):
+            bank = pmisc.tile([P, 4, P], F32, name="bank", tag="misc")
+            for g in range(2):
+                for u in range(2):
+                    nc.tensor.transpose(bank[:, 2 * g + u, :], src_words[:, 256 * g + u : 256 * (g + 1) : 2], ident[:])
+            return bank
+
+        def copy_turned(engine, bank, dst_words):
+            src = bank[:].rearrange("p (g u) b -> p g b u", g=2)
+            dst = dst_words.rearrange("p (g b u) -> p g b u", g=2, u=2)
+            if engine == "v":
+                nc.vector.tensor_copy(out=dst, in_=src)
+            else:
+                nc.scalar.copy(out=dst, in_=src)
+
+        def group(i, k, engine):
+            if i not in groups:
+                groups[i] = work.tile([P, MATS, 2 * P * 4], BF16, name="grouped", align_bytes=64)
+            bank = turn(nats[i][:, k, :].bitcast(F32))
+            copy_turned(engine, bank, groups[i][:, k, :].bitcast(F32))
+
+        def quantize_mat(i):
+            cd = work.tile([P, MATS, 2, P], U32, name="cd", align_bytes=64)
+            pn = work.tile([P, MATS, 2, P], U8, name="pn", align_bytes=64)
+            nc.vector.quantize_mx(
+                out=cd[:].rearrange("p k g b -> p (k g b)").bitcast(FP8X4),
+                scales=pn[:].rearrange("p k g b -> p (k g b)"),
+                in_=groups[i][:].rearrange("p k n -> p (k n)"),
+            )
+            codes[i], planes[i] = cd, pn
+
+        def turn_y(i, engine):
+            yt = deep.tile([P, 2, P * 4], BF16, name="yturn")
+            bank = turn(ynat[i][:].bitcast(F32))
+            copy_turned(engine, bank, yt[:].rearrange("p g n -> p (g n)").bitcast(F32))
+            yturned[i] = yt
+
+        lines, seconds, energies, parts = {}, {}, {}, {}
+
+        def integrate(i, h):
+            cols = slice(512 * h, 512 * (h + 1))
+            for k in (1, 0):
+                bank = pl.tile([P, 512], F32, name="line")
+                for g in range(2):
+                    nc.tensor.matmul_mx(
+                        out=bank[:],
+                        lhsT=codes[i][:, k, g, :].bitcast(FP8X4),
+                        lhsT_scale=planes[i][:, k, g, :],
+                        rhs=a_sb[:, g, 1024 * h : 1024 * (h + 1)].bitcast(FP4X4),
+                        rhs_scale=a_sc[:, g, cols],
+                        start=(g == 0),
+                        stop=(g == 1),
+                    )
+                lines[i, h, k] = bank
+
+        def copy_second(i, h):
+            second = work.tile([P, 4, P], F32, name="second")
+            nc.scalar.copy(out=second[:], in_=lines[i, h, 1][:].rearrange("b (c t) -> b t c", t=4))
+            seconds[i, h] = second
+
+        def argument(i, h, e):
+            if e == 0:
+                energies[i, h] = deep.tile([P, E, 4, P], F32, name="en")
+                parts[i, h] = deep.tile([P, 3, 3, 4 * P], F32, name="pt")
+            nc.vector.scalar_tensor_tensor(
+                out=energies[i, h][:, e],
+                in0=seconds[i, h][:],
+                scalar=rho[:, e : e + 1],
+                in1=lines[i, h, 0][:].rearrange("b (c t) -> b t c", t=4),
+                op0=ALU.mult,
+                op1=ALU.add,
+            )
+
+        def exponential(i, h, e):
+            en = energies[i, h]
+            nc.scalar.activation(out=en[:, e], in_=en[:, e], func=ACT.Exp, scale=neg[:, e : e + 1])
+
+        def product(i, h, e, j):
+            src = energies[i, h][:, e].rearrange("b t c -> b (t c)")
+            dst = parts[i, h][:, j, e - 1, :]
+            if (e, j) in POOL_PRODUCTS:
+                nc.gpsimd.tensor_scalar(
+                    out=dst, in0=src, scalar1=coef[:, j, e : e + 1], scalar2=0.0, op0=ALU.mult, op1=ALU.add
+                )
+            elif (e, j) in SCALAR_PRODUCTS:
+                nc.scalar.activation(out=dst, in_=src, func=ACT.Copy, scale=coef[:, j, e : e + 1])
+            else:
+                nc.vector.tensor_scalar(out=dst, in0=src, scalar1=coef[:, j, e : e + 1], scalar2=None, op0=ALU.mult)
+
+        def products(i, h, e):
+            for j in range(3):
+                product(i, h, e, j)
+
+        def pool_products(i, h, e):
+            for j in range(3):
+                if (e, j) in POOL_PRODUCTS:
+                    product(i, h, e, j)
+
+        def vector_products(i, h):
+            for j in range(3):
+                for e in range(1, E):
+                    if (e, j) not in POOL_PRODUCTS:
+                        product(i, h, e, j)
+
+        sums = {}
+
+        def add_up(i, h, j):
+            z = pz.tile([P, 4, P], F32, name="z")
+            for t in range(4):
+                for e in range(E):
+                    src = energies[i, h][:, 0, t, :] if e == 0 else parts[i, h][:, j, e - 1, P * t : P * (t + 1)]
+                    nc.tensor.matmul(
+                        out=z[:, t, :], lhsT=src, rhs=ident[:], is_transpose=True, start=(e == 0), stop=(e == E - 1)
+                    )
+            sums[i, h, j] = z[:].rearrange("p t b -> p b t")
+
+        recs, diffs, facs, gts, back_codes, back_planes, results = {}, {}, {}, {}, {}, {}, {}
+
+        def invert(i, h):
+            rec = work.tile([P, P, 4], F32, name="rec")
+            nc.vector.reciprocal(out=rec[:], in_=sums[i, h, 0])
+            recs[i, h] = rec
+
+        def ratio(i, h):
+            rat = work.tile([P, P, 4], F32, name="rat")
+            ys = yturned[i][:, h, :].rearrange("p (b t) -> p b t", t=4)
+            (nc.vector if (i, h) == (TILES - 1, 1) else nc.gpsimd).tensor_tensor(out=rat[:], in0=ys, in1=recs[i, h][:], op=ALU.mult)
+            diffs[i, h] = rat
+
+        def factor(i, h):
+            fac = work.tile([P, P, 4], F32, name="fac")
+            nc.vector.scalar_tensor_tensor(
+                out=fac[:],
+                in0=diffs[i, h][:],
+                scalar=lead[:, 4:5],
+                in1=w_sb[:, h, :].unsqueeze(1).to_broadcast([P, P, 4]),
+                op0=ALU.subtract,
+                op1=ALU.mult,
+            )
+            facs[i, h] = fac
+
+        def gradient(i, h, k):
+            if k == 0:
+                gts[i, h] = work.tile([P, MATS, P, 4], BF16, name="gt", align_bytes=64)
+            nc.vector.scalar_tensor_tensor(
+                out=gts[i, h][:, k],
+                in0=sums[i, h, 1 + k],
+                scalar=gsc[:, k : k + 1],
+                in1=facs[i, h][:],
+                op0=ALU.mult,
+                op1=ALU.mult,
+            )
+
+        def quantize_gradient(i, h):
+            cd = deep.tile([P, MATS, P], U32, name="bcd", align_bytes=64)
+            pn = deep.tile([P, MATS, P], U8, name="bpn", align_bytes=64)
+            nc.vector.quantize_mx(
+                out=cd[:].rearrange("p k b -> p (k b)").bitcast(FP8X4),
+                scales=pn[:].rearrange("p k b -> p (k b)"),
+                in_=gts[i, h][:].rearrange("p k b t -> p (k b t)"),
+            )
+            back_codes[i, h], back_planes[i, h] = cd, pn
+
+        def project(i, k, nh, engine):
+            if nh == 0:
+                results[i, k] = work.tile([P, N], F32, name="ores")
+            res = results[i, k]
+            cols = slice(512 * nh, 512 * (nh + 1))
+            bank = pmisc.tile([P, 512], F32, name="obank", tag="misc")
+            for h in range(2):
+                nc.tensor.matmul_mx(
+                    out=bank[:],
+                    lhsT=back_codes[i, h][:, k, :].bitcast(FP8X4),
+                    lhsT_scale=back_planes[i, h][:, k, :],
+                    rhs=q_sb[:, h, 1024 * nh : 1024 * (nh + 1)].bitcast(FP4X4),
+                    rhs_scale=q_sc[:, h, cols],
+                    start=(h == 0),
+                    stop=(h == 1),
+                )
+            if engine == "a":
+                nc.scalar.copy(out=res[:, cols], in_=bank[:])
+            else:
+                nc.vector.tensor_copy(out=res[:, cols], in_=bank[:])
+            if nh == 1:
+                nc.sync.dma_start(out=out[k, P * i : P * (i + 1), :], in_=res[:])
+
+        coefficients()
+        widen(0, 1, "a")
+        widen(0, 0, "v")
+        group(0, 1, "a")
+        group(0, 0, "v")
+        quantize_mat(0)
+        integrate(0, 0)
+        copy_second(0, 0)
+
+        def prepare(i):
+            widen(i, 1, "a" if i > 1 else "v")
+            widen(i, 0, "a" if i > 1 else "v")
+            group(i, 1, "a" if i > 1 else "v")
+            group(i, 0, "a")
+            quantize_mat(i)
+
+        def backward(i, h):
+            add_up(i, h, 0)
+            invert(i, h)
+            ratio(i, h)
+            add_up(i, h, 1)
+            add_up(i, h, 2)
+            factor(i, h)
+            gradient(i, h, 0)
+            gradient(i, h, 1)
+            quantize_gradient(i, h)
+
+        units = [(i, h) for i in range(TILES) for h in range(2)]
+        for n, (i, h) in enumerate(units):
+            for e in range(E):
+                argument(i, h, e)
+                exponential(i, h, e)
+            if h == 0 and i + 1 < TILES:
+                prepare(i + 1)
+            if n + 1 < len(units):
+                integrate(*units[n + 1])
+                copy_second(*units[n + 1])
+            if h == 0:
+                turn_y(i, "a")
+            for e in range(1, E):
+                products(i, h, e)
+            if n >= 1:
+                backward(*units[n - 1])
+            if h == 1 and i >= 1:
+                for k in range(MATS):
+                    for nh in range(2):
+                        project(i - 1, k, nh, "a"[nh % 1])
+        backward(*units[-1])
+        for k in range(MATS):
+            for nh in range(2):
+                project(TILES - 1, k, nh, "av"[nh])

@@ -20,8 +20,73 @@ ACT = mybir.ActivationFunctionType
 P = 128
 TILES = B // P
 TINY = 2.0**-100
-POOL_PRODUCTS = ((1, 0), (1, 1), (1, 2), (2, 0), (2, 1), (2, 2))
-SCALAR_PRODUCTS = ((3, 0), (3, 1), (3, 2))
+MISC_BANKS, LINE_BANKS, SUM_BANKS = 2, 3, 3
+WIDEN = [["aa","vv"],["vv","av"],["va","av"],["va","av"]]
+DRAIN = [["a","a","a"],["a","a","a"],["a","a","a"],["a","a","a"]]
+SECOND = "a"
+RATIO = "pppppppv"
+FACTOR = "aaaaaaav"
+STORE = ["aaaa","aaaa","aaaa","avav"]
+PRODUCT = [["ppp","ppp","vpa"],["pap","ppp","apa"],["pap","ppp","apa"],["pap","ppp","apa"],["pap","ppp","apa"],["pap","ppp","apa"],["pap","ppp","apa"],["paa","ava","paa"]]
+FIRST, LAST = -4, 13
+ORDER = (
+    ("grad0", 3),
+    ("inv", 2),
+    ("turny", -1),
+    ("out10", 5),
+    ("prod20", 1),
+    ("exp3", 1),
+    ("sum1", 2),
+    ("turn1", -2),
+    ("prod10", 1),
+    ("exp0", 1),
+    ("arg1", 0),
+    ("quant0", 3),
+    ("prod30", 1),
+    ("drain1", -2),
+    ("prod32", 2),
+    ("drain0", -1),
+    ("ratio", 2),
+    ("prod22", 2),
+    ("grad1", 3),
+    ("line1", -1),
+    ("out11", 5),
+    ("widen10", -3),
+    ("prod31", 1),
+    ("early10", 4),
+    ("early00", 3),
+    ("arg2", 0),
+    ("sum0", 1),
+    ("factor", 2),
+    ("quant1", 3),
+    ("prod11", 1),
+    ("widen11", -4),
+    ("arg3", 0),
+    ("second", -1),
+    ("late00", 3),
+    ("drainy", -1),
+    ("exp2", 0),
+    ("quantmat0", -1),
+    ("late10", 4),
+    ("quantmat1", -2),
+    ("exp1", 0),
+    ("widen01", -3),
+    ("widen00", -3),
+    ("out00", 3),
+    ("early01", 3),
+    ("early11", 4),
+    ("line0", -1),
+    ("late01", 3),
+    ("coefs", -3),
+    ("prod21", 1),
+    ("late11", 4),
+    ("sum2", 2),
+    ("out01", 3),
+    ("turn0", -2),
+    ("prod12", 1),
+    ("arg0", 0),
+    ("weights", -2),
+)
 
 
 def tile_polyenergetictwomaterialunmatchedbackpro_d1p_kernel(
@@ -33,9 +98,10 @@ def tile_polyenergetictwomaterialunmatchedbackpro_d1p_kernel(
         load = ctx.enter_context(tc.tile_pool(name="load", bufs=4))
         work = ctx.enter_context(tc.tile_pool(name="work", bufs=2))
         deep = ctx.enter_context(tc.tile_pool(name="deep", bufs=3))
-        pmisc = ctx.enter_context(tc.psum_pool(name="pmisc", bufs=2))
-        pl = ctx.enter_context(tc.psum_pool(name="pl", bufs=3))
-        pz = ctx.enter_context(tc.psum_pool(name="pz", bufs=3))
+        pmisc = ctx.enter_context(tc.psum_pool(name="pmisc", bufs=MISC_BANKS))
+        pl = ctx.enter_context(tc.psum_pool(name="pl", bufs=LINE_BANKS))
+        pz = ctx.enter_context(tc.psum_pool(name="pz", bufs=SUM_BANKS))
+        ctx.enter_context(tc.manual_schedule())
 
         ident = keep.tile([P, P], F32, name="ident")
         make_identity(nc, ident[:])
@@ -49,6 +115,7 @@ def tile_polyenergetictwomaterialunmatchedbackpro_d1p_kernel(
         warm = keep.tile([P, 1], F32, name="warm")
         nc.vector.memset(warm[:], 0.0)
         nc.scalar.activation(out=warm[:], in_=warm[:], func=ACT.Exp)
+
         raw, scl, ynat = [], [], []
 
         def load_mat(i):
@@ -72,11 +139,11 @@ def tile_polyenergetictwomaterialunmatchedbackpro_d1p_kernel(
                     in_=src[:, 4 * q : 4 * q + 4, :].bitcast(I32).rearrange("g r n -> r g n"),
                 )
 
-        load_mat(0)
         f_bf = keep.tile([P, MATS * E], BF16, name="f_bf")
         nc.sync.dma_start(out=f_bf[:], in_=f.rearrange("k e -> (k e)").partition_broadcast(P))
         s_bf = keep.tile([P, E], BF16, name="s_bf")
         nc.sync.dma_start(out=s_bf[:], in_=s.partition_broadcast(P))
+        load_mat(0)
         load_scales(a_sc, a_scales)
         for g in range(2):
             nc.sync.dma_start(out=a_sb[:, g, :].bitcast(I32), in_=a_words[g].bitcast(I32))
@@ -102,8 +169,10 @@ def tile_polyenergetictwomaterialunmatchedbackpro_d1p_kernel(
         inv = keep.tile([P, 7], F32, name="inv")
         rho = keep.tile([P, E], F32, name="rho")
         neg = keep.tile([P, 7], F32, name="neg")
-        gsc = keep.tile([P, MATS], F32, name="gsc")
         coef = keep.tile([P, 3, E], F32, name="coef")
+        gsc = keep.tile([P, MATS], F32, name="gsc")
+        w_up = keep.tile([P, 2, 4], F32, name="w_up")
+        w_down = keep.tile([P, 2, 4], F32, name="w_down")
 
         def coefficients():
             nc.vector.tensor_copy(out=fx[:], in_=f_bf[:])
@@ -123,92 +192,109 @@ def tile_polyenergetictwomaterialunmatchedbackpro_d1p_kernel(
             nc.vector.reciprocal(out=inv[:], in_=lead[:])
             nc.vector.tensor_tensor(out=rho[:], in0=fx[:, 4:8], in1=inv[:, 0:4], op=ALU.mult)
             nc.vector.tensor_scalar(out=neg[:], in0=lead[:], scalar1=-1.0, scalar2=None, op0=ALU.mult)
-            nc.vector.tensor_scalar(out=gsc[:], in0=neg[:, 5:7], scalar1=inv[:, 4:5], scalar2=None, op0=ALU.mult)
             nc.vector.tensor_scalar(out=coef[:, 0, :], in0=sx[:], scalar1=inv[:, 4:5], scalar2=None, op0=ALU.mult)
             for k in range(MATS):
                 nc.vector.tensor_scalar(
                     out=coef[:, 1 + k, :], in0=fs[:, k, :], scalar1=inv[:, 5 + k : 6 + k], scalar2=None, op0=ALU.mult
                 )
+            nc.vector.tensor_scalar(out=gsc[:], in0=neg[:, 5:7], scalar1=inv[:, 4:5], scalar2=None, op0=ALU.mult)
 
+        def weights():
+            nc.vector.tensor_copy(out=w_up[:], in_=w_sb[:])
+            nc.vector.tensor_scalar(
+                out=w_down[:], in0=w_up[:], scalar1=neg[:, 4:5], scalar2=None, op0=ALU.mult
+            )
 
         nats, groups, codes, planes, yturned = {}, {}, {}, {}, {}
+        banks = {}
+        lines, seconds, energies, parts = {}, {}, {}, {}
+        sums, recs, rats, facs, gts, back_codes, back_planes, results = {}, {}, {}, {}, {}, {}, {}, {}
 
-        def widen(i, k, engine):
+        def on(engine):
+            return {"v": nc.vector, "p": nc.gpsimd}[engine]
+
+        def move(engine, dst, src):
+            if engine == "a":
+                nc.scalar.copy(out=dst, in_=src)
+            else:
+                nc.vector.tensor_copy(out=dst, in_=src)
+
+        def widen(i, k, half):
             if i not in nats:
                 nats[i] = work.tile([P, MATS, N], BF16, name="nat")
             nat = nats[i]
-            for j in range(8):
+            for j in range(4 * half, 4 * half + 4):
                 cols = slice(P * j, P * (j + 1))
                 src = raw[i][:, k, cols].bitcast(FP8)
-                if engine == "a":
+                if WIDEN[i][k][half] == "a":
                     nc.scalar.activation(out=nat[:, k, cols], in_=src, func=ACT.Copy, scale=scl[i][:, k, j : j + 1])
                 else:
                     nc.vector.tensor_scalar(
                         out=nat[:, k, cols], in0=src, scalar1=scl[i][:, k, j : j + 1], scalar2=None, op0=ALU.mult
                     )
 
-        def turn(src_words):
+        def turn(key, src_words):
             bank = pmisc.tile([P, 4, P], F32, name="bank", tag="misc")
             for g in range(2):
-                for u in range(2):
-                    nc.tensor.transpose(bank[:, 2 * g + u, :], src_words[:, 256 * g + u : 256 * (g + 1) : 2], ident[:])
-            return bank
+                for v in range(2):
+                    nc.tensor.transpose(bank[:, 2 * g + v, :], src_words[:, 256 * g + v : 256 * (g + 1) : 2], ident[:])
+            banks[key] = bank
 
-        def copy_turned(engine, bank, dst_words):
-            src = bank[:].rearrange("p (g u) b -> p g b u", g=2)
-            dst = dst_words.rearrange("p (g b u) -> p g b u", g=2, u=2)
-            if engine == "v":
-                nc.vector.tensor_copy(out=dst, in_=src)
-            else:
-                nc.scalar.copy(out=dst, in_=src)
+        def drain(key, engine, dst_words):
+            move(
+                engine,
+                dst_words.rearrange("p (g b v) -> p g b v", g=2, v=2),
+                banks[key][:].rearrange("p (g v) b -> p g b v", g=2),
+            )
 
-        def group(i, k, engine):
+        def turn_mat(i, k):
+            turn((i, k), nats[i][:, k, :].bitcast(F32))
+
+        def drain_mat(i, k):
             if i not in groups:
                 groups[i] = work.tile([P, MATS, 2 * P * 4], BF16, name="grouped", align_bytes=64)
-            bank = turn(nats[i][:, k, :].bitcast(F32))
-            copy_turned(engine, bank, groups[i][:, k, :].bitcast(F32))
+            drain((i, k), DRAIN[i][k], groups[i][:, k, :].bitcast(F32))
 
-        def quantize_mat(i):
-            cd = work.tile([P, MATS, 2, P], U32, name="cd", align_bytes=64)
-            pn = work.tile([P, MATS, 2, P], U8, name="pn", align_bytes=64)
+        def quantize_mat(i, k):
+            if i not in codes:
+                codes[i] = work.tile([P, MATS, 2, P], U32, name="cd", align_bytes=64)
+                planes[i] = work.tile([P, MATS, 2, P], U8, name="pn", align_bytes=64)
             nc.vector.quantize_mx(
-                out=cd[:].rearrange("p k g b -> p (k g b)").bitcast(FP8X4),
-                scales=pn[:].rearrange("p k g b -> p (k g b)"),
-                in_=groups[i][:].rearrange("p k n -> p (k n)"),
+                out=codes[i][:, k].rearrange("p g b -> p (g b)").bitcast(FP8X4),
+                scales=planes[i][:, k].rearrange("p g b -> p (g b)"),
+                in_=groups[i][:, k, :],
             )
-            codes[i], planes[i] = cd, pn
 
-        def turn_y(i, engine):
+        def turn_y(i):
+            turn((i, 2), ynat[i][:].bitcast(F32))
+
+        def drain_y(i):
             yt = deep.tile([P, 2, P * 4], BF16, name="yturn")
-            bank = turn(ynat[i][:].bitcast(F32))
-            copy_turned(engine, bank, yt[:].rearrange("p g n -> p (g n)").bitcast(F32))
+            drain((i, 2), DRAIN[i][2], yt[:].rearrange("p g n -> p (g n)").bitcast(F32))
             yturned[i] = yt
 
-        lines, seconds, energies, parts = {}, {}, {}, {}
-
-        def integrate(i, h):
+        def line(i, h, k):
             cols = slice(512 * h, 512 * (h + 1))
-            for k in (1, 0):
-                bank = pl.tile([P, 512], F32, name="line")
-                for g in range(2):
-                    nc.tensor.matmul_mx(
-                        out=bank[:],
-                        lhsT=codes[i][:, k, g, :].bitcast(FP8X4),
-                        lhsT_scale=planes[i][:, k, g, :],
-                        rhs=a_sb[:, g, 1024 * h : 1024 * (h + 1)].bitcast(FP4X4),
-                        rhs_scale=a_sc[:, g, cols],
-                        start=(g == 0),
-                        stop=(g == 1),
-                    )
-                lines[i, h, k] = bank
+            bank = pl.tile([P, 512], F32, name="line", tag="line")
+            for g in range(2):
+                nc.tensor.matmul_mx(
+                    out=bank[:],
+                    lhsT=codes[i][:, k, g, :].bitcast(FP8X4),
+                    lhsT_scale=planes[i][:, k, g, :],
+                    rhs=a_sb[:, g, 1024 * h : 1024 * (h + 1)].bitcast(FP4X4),
+                    rhs_scale=a_sc[:, g, cols],
+                    start=(g == 0),
+                    stop=(g == 1),
+                )
+            lines[i, h, k] = bank
 
-        def copy_second(i, h):
-            second = work.tile([P, 4, P], F32, name="second")
-            nc.scalar.copy(out=second[:], in_=lines[i, h, 1][:].rearrange("b (c t) -> b t c", t=4))
-            seconds[i, h] = second
+        def second(i, h):
+            sec = work.tile([P, 4, P], F32, name="sec")
+            move(SECOND, sec[:], lines[i, h, 1][:].rearrange("b (c t) -> b t c", t=4))
+            seconds[i, h] = sec
 
         def argument(i, h, e):
-            if e == 0:
+            if (i, h) not in energies:
                 energies[i, h] = deep.tile([P, E, 4, P], F32, name="en")
                 parts[i, h] = deep.tile([P, 3, 3, 4 * P], F32, name="pt")
             nc.vector.scalar_tensor_tensor(
@@ -227,31 +313,15 @@ def tile_polyenergetictwomaterialunmatchedbackpro_d1p_kernel(
         def product(i, h, e, j):
             src = energies[i, h][:, e].rearrange("b t c -> b (t c)")
             dst = parts[i, h][:, j, e - 1, :]
-            if (e, j) in POOL_PRODUCTS:
+            engine = PRODUCT[2 * i + h][e - 1][j]
+            if engine == "a":
+                nc.scalar.activation(out=dst, in_=src, func=ACT.Copy, scale=coef[:, j, e : e + 1])
+            elif engine == "p":
                 nc.gpsimd.tensor_scalar(
                     out=dst, in0=src, scalar1=coef[:, j, e : e + 1], scalar2=0.0, op0=ALU.mult, op1=ALU.add
                 )
-            elif (e, j) in SCALAR_PRODUCTS:
-                nc.scalar.activation(out=dst, in_=src, func=ACT.Copy, scale=coef[:, j, e : e + 1])
             else:
                 nc.vector.tensor_scalar(out=dst, in0=src, scalar1=coef[:, j, e : e + 1], scalar2=None, op0=ALU.mult)
-
-        def products(i, h, e):
-            for j in range(3):
-                product(i, h, e, j)
-
-        def pool_products(i, h, e):
-            for j in range(3):
-                if (e, j) in POOL_PRODUCTS:
-                    product(i, h, e, j)
-
-        def vector_products(i, h):
-            for j in range(3):
-                for e in range(1, E):
-                    if (e, j) not in POOL_PRODUCTS:
-                        product(i, h, e, j)
-
-        sums = {}
 
         def add_up(i, h, j):
             z = pz.tile([P, 4, P], F32, name="z")
@@ -263,8 +333,6 @@ def tile_polyenergetictwomaterialunmatchedbackpro_d1p_kernel(
                     )
             sums[i, h, j] = z[:].rearrange("p t b -> p b t")
 
-        recs, diffs, facs, gts, back_codes, back_planes, results = {}, {}, {}, {}, {}, {}, {}
-
         def invert(i, h):
             rec = work.tile([P, P, 4], F32, name="rec")
             nc.vector.reciprocal(out=rec[:], in_=sums[i, h, 0])
@@ -272,24 +340,38 @@ def tile_polyenergetictwomaterialunmatchedbackpro_d1p_kernel(
 
         def ratio(i, h):
             rat = work.tile([P, P, 4], F32, name="rat")
-            ys = yturned[i][:, h, :].rearrange("p (b t) -> p b t", t=4)
-            (nc.vector if (i, h) == (TILES - 1, 1) else nc.gpsimd).tensor_tensor(out=rat[:], in0=ys, in1=recs[i, h][:], op=ALU.mult)
-            diffs[i, h] = rat
+            on(RATIO[2 * i + h]).tensor_tensor(
+                out=rat[:],
+                in0=yturned[i][:, h, :].rearrange("p (b t) -> p b t", t=4),
+                in1=recs[i, h][:],
+                op=ALU.mult,
+            )
+            rats[i, h] = rat
 
         def factor(i, h):
             fac = work.tile([P, P, 4], F32, name="fac")
-            nc.vector.scalar_tensor_tensor(
-                out=fac[:],
-                in0=diffs[i, h][:],
-                scalar=lead[:, 4:5],
-                in1=w_sb[:, h, :].unsqueeze(1).to_broadcast([P, P, 4]),
-                op0=ALU.subtract,
-                op1=ALU.mult,
-            )
+            if FACTOR[2 * i + h] == "a":
+                for t in range(4):
+                    nc.scalar.activation(
+                        out=fac[:, :, t],
+                        in_=rats[i, h][:, :, t],
+                        func=ACT.Identity,
+                        scale=w_up[:, h, t : t + 1],
+                        bias=w_down[:, h, t : t + 1],
+                    )
+            else:
+                nc.vector.scalar_tensor_tensor(
+                    out=fac[:],
+                    in0=rats[i, h][:],
+                    scalar=lead[:, 4:5],
+                    in1=w_up[:, h, :].unsqueeze(1).to_broadcast([P, P, 4]),
+                    op0=ALU.subtract,
+                    op1=ALU.mult,
+                )
             facs[i, h] = fac
 
         def gradient(i, h, k):
-            if k == 0:
+            if (i, h) not in gts:
                 gts[i, h] = work.tile([P, MATS, P, 4], BF16, name="gt", align_bytes=64)
             nc.vector.scalar_tensor_tensor(
                 out=gts[i, h][:, k],
@@ -300,87 +382,83 @@ def tile_polyenergetictwomaterialunmatchedbackpro_d1p_kernel(
                 op1=ALU.mult,
             )
 
-        def quantize_gradient(i, h):
-            cd = deep.tile([P, MATS, P], U32, name="bcd", align_bytes=64)
-            pn = deep.tile([P, MATS, P], U8, name="bpn", align_bytes=64)
+        def quantize_gradient(i, h, k):
+            if (i, h) not in back_codes:
+                back_codes[i, h] = deep.tile([P, MATS, P], U32, name="bcd", align_bytes=64)
+                back_planes[i, h] = deep.tile([P, MATS, P], U8, name="bpn", align_bytes=64)
             nc.vector.quantize_mx(
-                out=cd[:].rearrange("p k b -> p (k b)").bitcast(FP8X4),
-                scales=pn[:].rearrange("p k b -> p (k b)"),
-                in_=gts[i, h][:].rearrange("p k b t -> p (k b t)"),
+                out=back_codes[i, h][:, k, :].bitcast(FP8X4),
+                scales=back_planes[i, h][:, k, :],
+                in_=gts[i, h][:, k].rearrange("p b t -> p (b t)"),
             )
-            back_codes[i, h], back_planes[i, h] = cd, pn
 
-        def project(i, k, nh, engine):
-            if nh == 0:
-                results[i, k] = work.tile([P, N], F32, name="ores")
-            res = results[i, k]
-            cols = slice(512 * nh, 512 * (nh + 1))
-            bank = pmisc.tile([P, 512], F32, name="obank", tag="misc")
-            for h in range(2):
-                nc.tensor.matmul_mx(
-                    out=bank[:],
-                    lhsT=back_codes[i, h][:, k, :].bitcast(FP8X4),
-                    lhsT_scale=back_planes[i, h][:, k, :],
-                    rhs=q_sb[:, h, 1024 * nh : 1024 * (nh + 1)].bitcast(FP4X4),
-                    rhs_scale=q_sc[:, h, cols],
-                    start=(h == 0),
-                    stop=(h == 1),
-                )
-            if engine == "a":
-                nc.scalar.copy(out=res[:, cols], in_=bank[:])
-            else:
-                nc.vector.tensor_copy(out=res[:, cols], in_=bank[:])
-            if nh == 1:
-                nc.sync.dma_start(out=out[k, P * i : P * (i + 1), :], in_=res[:])
-
-        coefficients()
-        widen(0, 1, "a")
-        widen(0, 0, "v")
-        group(0, 1, "a")
-        group(0, 0, "v")
-        quantize_mat(0)
-        integrate(0, 0)
-        copy_second(0, 0)
-
-        def prepare(i):
-            widen(i, 1, "a" if i > 1 else "v")
-            widen(i, 0, "a" if i > 1 else "v")
-            group(i, 1, "a" if i > 1 else "v")
-            group(i, 0, "a")
-            quantize_mat(i)
-
-        def backward(i, h):
-            add_up(i, h, 0)
-            invert(i, h)
-            ratio(i, h)
-            add_up(i, h, 1)
-            add_up(i, h, 2)
-            factor(i, h)
-            gradient(i, h, 0)
-            gradient(i, h, 1)
-            quantize_gradient(i, h)
-
-        units = [(i, h) for i in range(TILES) for h in range(2)]
-        for n, (i, h) in enumerate(units):
-            for e in range(E):
-                argument(i, h, e)
-                exponential(i, h, e)
-            if h == 0 and i + 1 < TILES:
-                prepare(i + 1)
-            if n + 1 < len(units):
-                integrate(*units[n + 1])
-                copy_second(*units[n + 1])
+        def project(i, k, nh, h):
             if h == 0:
-                turn_y(i, "a")
-            for e in range(1, E):
-                products(i, h, e)
-            if n >= 1:
-                backward(*units[n - 1])
-            if h == 1 and i >= 1:
-                for k in range(MATS):
-                    for nh in range(2):
-                        project(i - 1, k, nh, "a"[nh % 1])
-        backward(*units[-1])
+                if i == TILES - 1 and nh == 1:
+                    results[i, k, nh] = pl.tile([P, 512], F32, name="lastbank", tag="line")
+                else:
+                    results[i, k, nh] = pmisc.tile([P, 512], F32, name="obank", tag="misc")
+            nc.tensor.matmul_mx(
+                out=results[i, k, nh][:],
+                lhsT=back_codes[i, h][:, k, :].bitcast(FP8X4),
+                lhsT_scale=back_planes[i, h][:, k, :],
+                rhs=q_sb[:, h, 1024 * nh : 1024 * (nh + 1)].bitcast(FP4X4),
+                rhs_scale=q_sc[:, h, 512 * nh : 512 * (nh + 1)],
+                start=(h == 0),
+                stop=(h == 1),
+            )
+
+        def early(i, k, nh):
+            if i == TILES - 1:
+                project(i, k, nh, 0)
+
+        def late(i, k, nh):
+            if i < TILES - 1:
+                project(i, k, nh, 0)
+            project(i, k, nh, 1)
+
+        def store(i, k, nh):
+            res = load.tile([P, 512], F32, name="ores")
+            move(STORE[i][2 * k + nh], res[:], results[i, k, nh][:])
+            nc.sync.dma_start(out=out[k, P * i : P * (i + 1), 512 * nh : 512 * (nh + 1)], in_=res[:])
+
+        def tile_stage(fn, *rest):
+            return lambda n: fn(n // 2, *rest) if n % 2 == 0 else None
+
+        def last_stage(fn, *rest):
+            return lambda n: fn(n // 2, *rest) if n % 2 == 1 else None
+
+        def unit_stage(fn, *rest):
+            return lambda n: fn(n // 2, n % 2, *rest)
+
+        stages = {"coefs": lambda n: coefficients() if n == 0 else None, "weights": lambda n: weights() if n == 0 else None, "turny": tile_stage(turn_y), "drainy": tile_stage(drain_y)}
         for k in range(MATS):
+            stages["quantmat%d" % k] = tile_stage(quantize_mat, k)
+            stages["quant%d" % k] = unit_stage(quantize_gradient, k)
+            for half in range(2):
+                stages["widen%d%d" % (k, half)] = tile_stage(widen, k, half)
+            stages["turn%d" % k] = tile_stage(turn_mat, k)
+            stages["drain%d" % k] = tile_stage(drain_mat, k)
+            stages["line%d" % k] = unit_stage(line, k)
+            stages["grad%d" % k] = unit_stage(gradient, k)
             for nh in range(2):
-                project(TILES - 1, k, nh, "av"[nh])
+                stages["early%d%d" % (k, nh)] = last_stage(early, k, nh)
+                stages["late%d%d" % (k, nh)] = last_stage(late, k, nh)
+                stages["out%d%d" % (k, nh)] = last_stage(store, k, nh)
+        for e in range(E):
+            stages["arg%d" % e] = unit_stage(argument, e)
+            stages["exp%d" % e] = unit_stage(exponential, e)
+            for j in range(3):
+                if e:
+                    stages["prod%d%d" % (e, j)] = unit_stage(product, e, j)
+        for j in range(3):
+            stages["sum%d" % j] = unit_stage(add_up, j)
+        stages["second"] = unit_stage(second)
+        stages["inv"] = unit_stage(invert)
+        stages["ratio"] = unit_stage(ratio)
+        stages["factor"] = unit_stage(factor)
+
+        for step in range(FIRST, LAST):
+            for name, lag in ORDER:
+                if 0 <= step - lag < 2 * TILES:
+                    stages[name](step - lag)

from contextlib import ExitStack

import concourse.mybir as mybir
from concourse.masks import make_identity

MATS, B, N, M, E = 2, 512, 1024, 1024, 4
FLOPS = 2 * 2 * MATS * B * N * M

F32 = mybir.dt.float32
BF16 = mybir.dt.bfloat16
I32 = mybir.dt.int32
U32 = mybir.dt.uint32
U8 = mybir.dt.uint8
FP8 = mybir.dt.float8_e4m3fn
FP8X4 = mybir.dt.float8_e4m3fn_x4
FP4X4 = mybir.dt.float4_e2m1fn_x4
ALU = mybir.AluOpType
ACT = mybir.ActivationFunctionType

P = 128
TILES = B // P
TINY = 2.0**-100
MISC_BANKS, LINE_BANKS, SUM_BANKS = 2, 3, 3
WIDEN = [["aa","vv"],["vv","av"],["va","av"],["va","av"]]
DRAIN = [["a","a","a"],["a","a","a"],["a","a","a"],["a","a","a"]]
SECOND = "a"
RATIO = "pppppppv"
FACTOR = "aaaaaaav"
STORE = ["aaaa","aaaa","aaaa","avav"]
PRODUCT = [["ppp","ppp","vpa"],["pap","ppp","apa"],["pap","ppp","apa"],["pap","ppp","apa"],["pap","ppp","apa"],["pap","ppp","apa"],["pap","ppp","apa"],["paa","ava","paa"]]
FIRST, LAST = -4, 13
ORDER = (
    ("grad0", 3),
    ("inv", 2),
    ("turny", -1),
    ("out10", 5),
    ("prod20", 1),
    ("exp3", 1),
    ("sum1", 2),
    ("turn1", -2),
    ("prod10", 1),
    ("exp0", 1),
    ("arg1", 0),
    ("quant0", 3),
    ("prod30", 1),
    ("drain1", -2),
    ("prod32", 2),
    ("drain0", -1),
    ("ratio", 2),
    ("prod22", 2),
    ("grad1", 3),
    ("line1", -1),
    ("out11", 5),
    ("widen10", -3),
    ("prod31", 1),
    ("early10", 4),
    ("early00", 3),
    ("arg2", 0),
    ("sum0", 1),
    ("factor", 2),
    ("quant1", 3),
    ("prod11", 1),
    ("widen11", -4),
    ("arg3", 0),
    ("second", -1),
    ("late00", 3),
    ("drainy", -1),
    ("exp2", 0),
    ("quantmat0", -1),
    ("late10", 4),
    ("quantmat1", -2),
    ("exp1", 0),
    ("widen01", -3),
    ("widen00", -3),
    ("out00", 3),
    ("early01", 3),
    ("early11", 4),
    ("line0", -1),
    ("late01", 3),
    ("coefs", -3),
    ("prod21", 1),
    ("late11", 4),
    ("sum2", 2),
    ("out01", 3),
    ("turn0", -2),
    ("prod12", 1),
    ("arg0", 0),
    ("weights", -2),
)


def tile_polyenergetictwomaterialunmatchedbackpro_d1p_kernel(
    tc, mat_bytes, mat_scale, a_words, a_scales, f, s, y, w, q_words, q_scales, out
):
    nc = tc.nc
    with ExitStack() as ctx:
        keep = ctx.enter_context(tc.tile_pool(name="keep", bufs=1))
        load = ctx.enter_context(tc.tile_pool(name="load", bufs=4))
        work = ctx.enter_context(tc.tile_pool(name="work", bufs=2))
        deep = ctx.enter_context(tc.tile_pool(name="deep", bufs=3))
        pmisc = ctx.enter_context(tc.psum_pool(name="pmisc", bufs=MISC_BANKS))
        pl = ctx.enter_context(tc.psum_pool(name="pl", bufs=LINE_BANKS))
        pz = ctx.enter_context(tc.psum_pool(name="pz", bufs=SUM_BANKS))
        ctx.enter_context(tc.manual_schedule())

        ident = keep.tile([P, P], F32, name="ident")
        make_identity(nc, ident[:])
        a_sc = keep.tile([P, 2, M], U8, name="a_sc", align_bytes=64)
        q_sc = keep.tile([P, 2, N], U8, name="q_sc", align_bytes=64)
        nc.vector.memset(a_sc[:].rearrange("p g n -> p (g n)").bitcast(I32), 0)
        nc.vector.memset(q_sc[:].rearrange("p g n -> p (g n)").bitcast(I32), 0)
        a_sb = keep.tile([P, 2, 2 * M], U8, name="a_sb", align_bytes=64)
        q_sb = keep.tile([P, 2, 2 * N], U8, name="q_sb", align_bytes=64)

        warm = keep.tile([P, 1], F32, name="warm")
        nc.vector.memset(warm[:], 0.0)
        nc.scalar.activation(out=warm[:], in_=warm[:], func=ACT.Exp)

        raw, scl, ynat = [], [], []

        def load_mat(i):
            rows = slice(P * i, P * (i + 1))
            sc = load.tile([P, MATS, 8], F32, name="sc")
            nc.sync.dma_start(out=sc[:], in_=mat_scale[:, rows, :].rearrange("k b j -> b k j"))
            rb = load.tile([P, MATS, N], U8, name="rb")
            nc.sync.dma_start(out=rb[:], in_=mat_bytes[:, rows, :].rearrange("k b n -> b k n"))
            scl.append(sc)
            raw.append(rb)

        def load_y(i):
            yt = load.tile([P, M], BF16, name="yt")
            nc.sync.dma_start(out=yt[:], in_=y[P * i : P * (i + 1), :])
            ynat.append(yt)

        def load_scales(dst, src):
            for q in range(4):
                nc.sync.dma_start(
                    out=dst[32 * q : 32 * q + 4, :, :].bitcast(I32),
                    in_=src[:, 4 * q : 4 * q + 4, :].bitcast(I32).rearrange("g r n -> r g n"),
                )

        f_bf = keep.tile([P, MATS * E], BF16, name="f_bf")
        nc.sync.dma_start(out=f_bf[:], in_=f.rearrange("k e -> (k e)").partition_broadcast(P))
        s_bf = keep.tile([P, E], BF16, name="s_bf")
        nc.sync.dma_start(out=s_bf[:], in_=s.partition_broadcast(P))
        load_mat(0)
        load_scales(a_sc, a_scales)
        for g in range(2):
            nc.sync.dma_start(out=a_sb[:, g, :].bitcast(I32), in_=a_words[g].bitcast(I32))
        load_mat(1)
        load_y(0)
        w_sb = keep.tile([P, 2, 4], BF16, name="w_sb")
        nc.sync.dma_start(out=w_sb[:], in_=w.rearrange("(g p t) -> p g t", g=2, t=4))
        load_scales(q_sc, q_scales)
        for g in range(2):
            nc.sync.dma_start(out=q_sb[:, g, :].bitcast(I32), in_=q_words[g].bitcast(I32))
        load_y(1)
        for i in range(2, TILES):
            load_mat(i)
            load_y(i)

        fx = keep.tile([P, MATS * E], F32, name="fx")
        sx = keep.tile([P, E], F32, name="sx")
        fs = keep.tile([P, MATS, E], F32, name="fs")
        norm = keep.tile([P, 7], F32, name="norm")
        mag = keep.tile([P, 7], F32, name="mag")
        bump = keep.tile([P, 7], F32, name="bump")
        lead = keep.tile([P, 7], F32, name="lead")
        inv = keep.tile([P, 7], F32, name="inv")
        rho = keep.tile([P, E], F32, name="rho")
        neg = keep.tile([P, 7], F32, name="neg")
        coef = keep.tile([P, 3, E], F32, name="coef")
        gsc = keep.tile([P, MATS], F32, name="gsc")
        w_up = keep.tile([P, 2, 4], F32, name="w_up")
        w_down = keep.tile([P, 2, 4], F32, name="w_down")

        def coefficients():
            nc.vector.tensor_copy(out=fx[:], in_=f_bf[:])
            nc.vector.tensor_copy(out=sx[:], in_=s_bf[:])
            nc.vector.tensor_tensor(
                out=fs[:],
                in0=fx[:].rearrange("p (k e) -> p k e", k=MATS),
                in1=sx[:].unsqueeze(1).to_broadcast([P, MATS, E]),
                op=ALU.mult,
            )
            nc.vector.tensor_copy(out=norm[:, 0:4], in_=fx[:, 0:4])
            nc.vector.tensor_copy(out=norm[:, 4:5], in_=sx[:, 0:1])
            nc.vector.tensor_copy(out=norm[:, 5:7], in_=fs[:, :, 0])
            nc.vector.scalar_tensor_tensor(out=mag[:], in0=norm[:], scalar=-1.0, in1=norm[:], op0=ALU.mult, op1=ALU.max)
            nc.vector.tensor_scalar(out=bump[:], in0=mag[:], scalar1=TINY, scalar2=TINY, op0=ALU.is_lt, op1=ALU.mult)
            nc.vector.tensor_tensor(out=lead[:], in0=norm[:], in1=bump[:], op=ALU.add)
            nc.vector.reciprocal(out=inv[:], in_=lead[:])
            nc.vector.tensor_tensor(out=rho[:], in0=fx[:, 4:8], in1=inv[:, 0:4], op=ALU.mult)
            nc.vector.tensor_scalar(out=neg[:], in0=lead[:], scalar1=-1.0, scalar2=None, op0=ALU.mult)
            nc.vector.tensor_scalar(out=coef[:, 0, :], in0=sx[:], scalar1=inv[:, 4:5], scalar2=None, op0=ALU.mult)
            for k in range(MATS):
                nc.vector.tensor_scalar(
                    out=coef[:, 1 + k, :], in0=fs[:, k, :], scalar1=inv[:, 5 + k : 6 + k], scalar2=None, op0=ALU.mult
                )
            nc.vector.tensor_scalar(out=gsc[:], in0=neg[:, 5:7], scalar1=inv[:, 4:5], scalar2=None, op0=ALU.mult)

        def weights():
            nc.vector.tensor_copy(out=w_up[:], in_=w_sb[:])
            nc.vector.tensor_scalar(
                out=w_down[:], in0=w_up[:], scalar1=neg[:, 4:5], scalar2=None, op0=ALU.mult
            )

        nats, groups, codes, planes, yturned = {}, {}, {}, {}, {}
        banks = {}
        lines, seconds, energies, parts = {}, {}, {}, {}
        sums, recs, rats, facs, gts, back_codes, back_planes, results = {}, {}, {}, {}, {}, {}, {}, {}

        def on(engine):
            return {"v": nc.vector, "p": nc.gpsimd}[engine]

        def move(engine, dst, src):
            if engine == "a":
                nc.scalar.copy(out=dst, in_=src)
            else:
                nc.vector.tensor_copy(out=dst, in_=src)

        def widen(i, k, half):
            if i not in nats:
                nats[i] = work.tile([P, MATS, N], BF16, name="nat")
            nat = nats[i]
            for j in range(4 * half, 4 * half + 4):
                cols = slice(P * j, P * (j + 1))
                src = raw[i][:, k, cols].bitcast(FP8)
                if WIDEN[i][k][half] == "a":
                    nc.scalar.activation(out=nat[:, k, cols], in_=src, func=ACT.Copy, scale=scl[i][:, k, j : j + 1])
                else:
                    nc.vector.tensor_scalar(
                        out=nat[:, k, cols], in0=src, scalar1=scl[i][:, k, j : j + 1], scalar2=None, op0=ALU.mult
                    )

        def turn(key, src_words):
            bank = pmisc.tile([P, 4, P], F32, name="bank", tag="misc")
            for g in range(2):
                for v in range(2):
                    nc.tensor.transpose(bank[:, 2 * g + v, :], src_words[:, 256 * g + v : 256 * (g + 1) : 2], ident[:])
            banks[key] = bank

        def drain(key, engine, dst_words):
            move(
                engine,
                dst_words.rearrange("p (g b v) -> p g b v", g=2, v=2),
                banks[key][:].rearrange("p (g v) b -> p g b v", g=2),
            )

        def turn_mat(i, k):
            turn((i, k), nats[i][:, k, :].bitcast(F32))

        def drain_mat(i, k):
            if i not in groups:
                groups[i] = work.tile([P, MATS, 2 * P * 4], BF16, name="grouped", align_bytes=64)
            drain((i, k), DRAIN[i][k], groups[i][:, k, :].bitcast(F32))

        def quantize_mat(i, k):
            if i not in codes:
                codes[i] = work.tile([P, MATS, 2, P], U32, name="cd", align_bytes=64)
                planes[i] = work.tile([P, MATS, 2, P], U8, name="pn", align_bytes=64)
            nc.vector.quantize_mx(
                out=codes[i][:, k].rearrange("p g b -> p (g b)").bitcast(FP8X4),
                scales=planes[i][:, k].rearrange("p g b -> p (g b)"),
                in_=groups[i][:, k, :],
            )

        def turn_y(i):
            turn((i, 2), ynat[i][:].bitcast(F32))

        def drain_y(i):
            yt = deep.tile([P, 2, P * 4], BF16, name="yturn")
            drain((i, 2), DRAIN[i][2], yt[:].rearrange("p g n -> p (g n)").bitcast(F32))
            yturned[i] = yt

        def line(i, h, k):
            cols = slice(512 * h, 512 * (h + 1))
            bank = pl.tile([P, 512], F32, name="line", tag="line")
            for g in range(2):
                nc.tensor.matmul_mx(
                    out=bank[:],
                    lhsT=codes[i][:, k, g, :].bitcast(FP8X4),
                    lhsT_scale=planes[i][:, k, g, :],
                    rhs=a_sb[:, g, 1024 * h : 1024 * (h + 1)].bitcast(FP4X4),
                    rhs_scale=a_sc[:, g, cols],
                    start=(g == 0),
                    stop=(g == 1),
                )
            lines[i, h, k] = bank

        def second(i, h):
            sec = work.tile([P, 4, P], F32, name="sec")
            move(SECOND, sec[:], lines[i, h, 1][:].rearrange("b (c t) -> b t c", t=4))
            seconds[i, h] = sec

        def argument(i, h, e):
            if (i, h) not in energies:
                energies[i, h] = deep.tile([P, E, 4, P], F32, name="en")
                parts[i, h] = deep.tile([P, 3, 3, 4 * P], F32, name="pt")
            nc.vector.scalar_tensor_tensor(
                out=energies[i, h][:, e],
                in0=seconds[i, h][:],
                scalar=rho[:, e : e + 1],
                in1=lines[i, h, 0][:].rearrange("b (c t) -> b t c", t=4),
                op0=ALU.mult,
                op1=ALU.add,
            )

        def exponential(i, h, e):
            en = energies[i, h]
            nc.scalar.activation(out=en[:, e], in_=en[:, e], func=ACT.Exp, scale=neg[:, e : e + 1])

        def product(i, h, e, j):
            src = energies[i, h][:, e].rearrange("b t c -> b (t c)")
            dst = parts[i, h][:, j, e - 1, :]
            engine = PRODUCT[2 * i + h][e - 1][j]
            if engine == "a":
                nc.scalar.activation(out=dst, in_=src, func=ACT.Copy, scale=coef[:, j, e : e + 1])
            elif engine == "p":
                nc.gpsimd.tensor_scalar(
                    out=dst, in0=src, scalar1=coef[:, j, e : e + 1], scalar2=0.0, op0=ALU.mult, op1=ALU.add
                )
            else:
                nc.vector.tensor_scalar(out=dst, in0=src, scalar1=coef[:, j, e : e + 1], scalar2=None, op0=ALU.mult)

        def add_up(i, h, j):
            z = pz.tile([P, 4, P], F32, name="z")
            for t in range(4):
                for e in range(E):
                    src = energies[i, h][:, 0, t, :] if e == 0 else parts[i, h][:, j, e - 1, P * t : P * (t + 1)]
                    nc.tensor.matmul(
                        out=z[:, t, :], lhsT=src, rhs=ident[:], is_transpose=True, start=(e == 0), stop=(e == E - 1)
                    )
            sums[i, h, j] = z[:].rearrange("p t b -> p b t")

        def invert(i, h):
            rec = work.tile([P, P, 4], F32, name="rec")
            nc.vector.reciprocal(out=rec[:], in_=sums[i, h, 0])
            recs[i, h] = rec

        def ratio(i, h):
            rat = work.tile([P, P, 4], F32, name="rat")
            on(RATIO[2 * i + h]).tensor_tensor(
                out=rat[:],
                in0=yturned[i][:, h, :].rearrange("p (b t) -> p b t", t=4),
                in1=recs[i, h][:],
                op=ALU.mult,
            )
            rats[i, h] = rat

        def factor(i, h):
            fac = work.tile([P, P, 4], F32, name="fac")
            if FACTOR[2 * i + h] == "a":
                for t in range(4):
                    nc.scalar.activation(
                        out=fac[:, :, t],
                        in_=rats[i, h][:, :, t],
                        func=ACT.Identity,
                        scale=w_up[:, h, t : t + 1],
                        bias=w_down[:, h, t : t + 1],
                    )
            else:
                nc.vector.scalar_tensor_tensor(
                    out=fac[:],
                    in0=rats[i, h][:],
                    scalar=lead[:, 4:5],
                    in1=w_up[:, h, :].unsqueeze(1).to_broadcast([P, P, 4]),
                    op0=ALU.subtract,
                    op1=ALU.mult,
                )
            facs[i, h] = fac

        def gradient(i, h, k):
            if (i, h) not in gts:
                gts[i, h] = work.tile([P, MATS, P, 4], BF16, name="gt", align_bytes=64)
            nc.vector.scalar_tensor_tensor(
                out=gts[i, h][:, k],
                in0=sums[i, h, 1 + k],
                scalar=gsc[:, k : k + 1],
                in1=facs[i, h][:],
                op0=ALU.mult,
                op1=ALU.mult,
            )

        def quantize_gradient(i, h, k):
            if (i, h) not in back_codes:
                back_codes[i, h] = deep.tile([P, MATS, P], U32, name="bcd", align_bytes=64)
                back_planes[i, h] = deep.tile([P, MATS, P], U8, name="bpn", align_bytes=64)
            nc.vector.quantize_mx(
                out=back_codes[i, h][:, k, :].bitcast(FP8X4),
                scales=back_planes[i, h][:, k, :],
                in_=gts[i, h][:, k].rearrange("p b t -> p (b t)"),
            )

        def project(i, k, nh, h):
            if h == 0:
                if i == TILES - 1 and nh == 1:
                    results[i, k, nh] = pl.tile([P, 512], F32, name="lastbank", tag="line")
                else:
                    results[i, k, nh] = pmisc.tile([P, 512], F32, name="obank", tag="misc")
            nc.tensor.matmul_mx(
                out=results[i, k, nh][:],
                lhsT=back_codes[i, h][:, k, :].bitcast(FP8X4),
                lhsT_scale=back_planes[i, h][:, k, :],
                rhs=q_sb[:, h, 1024 * nh : 1024 * (nh + 1)].bitcast(FP4X4),
                rhs_scale=q_sc[:, h, 512 * nh : 512 * (nh + 1)],
                start=(h == 0),
                stop=(h == 1),
            )

        def early(i, k, nh):
            if i == TILES - 1:
                project(i, k, nh, 0)

        def late(i, k, nh):
            if i < TILES - 1:
                project(i, k, nh, 0)
            project(i, k, nh, 1)

        def store(i, k, nh):
            res = load.tile([P, 512], F32, name="ores")
            move(STORE[i][2 * k + nh], res[:], results[i, k, nh][:])
            nc.sync.dma_start(out=out[k, P * i : P * (i + 1), 512 * nh : 512 * (nh + 1)], in_=res[:])

        def tile_stage(fn, *rest):
            return lambda n: fn(n // 2, *rest) if n % 2 == 0 else None

        def last_stage(fn, *rest):
            return lambda n: fn(n // 2, *rest) if n % 2 == 1 else None

        def unit_stage(fn, *rest):
            return lambda n: fn(n // 2, n % 2, *rest)

        stages = {"coefs": lambda n: coefficients() if n == 0 else None, "weights": lambda n: weights() if n == 0 else None, "turny": tile_stage(turn_y), "drainy": tile_stage(drain_y)}
        for k in range(MATS):
            stages["quantmat%d" % k] = tile_stage(quantize_mat, k)
            stages["quant%d" % k] = unit_stage(quantize_gradient, k)
            for half in range(2):
                stages["widen%d%d" % (k, half)] = tile_stage(widen, k, half)
            stages["turn%d" % k] = tile_stage(turn_mat, k)
            stages["drain%d" % k] = tile_stage(drain_mat, k)
            stages["line%d" % k] = unit_stage(line, k)
            stages["grad%d" % k] = unit_stage(gradient, k)
            for nh in range(2):
                stages["early%d%d" % (k, nh)] = last_stage(early, k, nh)
                stages["late%d%d" % (k, nh)] = last_stage(late, k, nh)
                stages["out%d%d" % (k, nh)] = last_stage(store, k, nh)
        for e in range(E):
            stages["arg%d" % e] = unit_stage(argument, e)
            stages["exp%d" % e] = unit_stage(exponential, e)
            for j in range(3):
                if e:
                    stages["prod%d%d" % (e, j)] = unit_stage(product, e, j)
        for j in range(3):
            stages["sum%d" % j] = unit_stage(add_up, j)
        stages["second"] = unit_stage(second)
        stages["inv"] = unit_stage(invert)
        stages["ratio"] = unit_stage(ratio)
        stages["factor"] = unit_stage(factor)

        for step in range(FIRST, LAST):
            for name, lag in ORDER:
                if 0 <= step - lag < 2 * TILES:
                    stages[name](step - lag)
